import numpy as np, ml_dtypes
CORES = [113,118,241,246]
N = 4
BF = ml_dtypes.bfloat16
def gentries(a):
    return np.ascontiguousarray(a.reshape(8, 16, -1).transpose(0, 2, 1)).reshape(8, -1)
def gtable(e):
    e = np.asarray(e); return np.ascontiguousarray(e.reshape(8, -1, 16).transpose(0, 2, 1)).reshape(128, -1).astype(np.int32)
B, W, F, R, L, S, ST, RO, CAP = 1472, 2240, 3, 384, 128, 3, 2, 2, 48
def points(rng, n):
    hub = rng.integers(0, B, (N, 8, 24))
    return np.where(rng.random((N, 8, n)) < 0.3, np.take_along_axis(hub, rng.integers(0, 24, (N, 8, n)), 2), rng.integers(0, B, (N, 8, n)))
def starts(rng, sizes):
    pool = np.argsort(rng.random((N, 8, B)), axis=-1)
    return np.take_along_axis(pool, (rng.random((N, 8, R)) * sizes).astype(np.int64), 2)
def backs(rng, v):
    return 4 * v + rng.integers(0, F, v.shape)
def fills(rng):
    share = rng.permutation(np.array([0.1, 0.3, 0.5, 0.7, 0.85, 0.9, 0.97, 1.0]))[:, None, None]
    return np.where(rng.random((N, 8, F, B)) < share, rng.integers(0, 7, (N, 8, F, B)), 7)
def parts(rng):
    x = rng.integers(0, 256, (N, 8, 16, B)); q = rng.integers(0, 256, (N, 8, 16, R))
    pf = points(rng, F * B).reshape(N, 8, F, B); mb = points(rng, F * B).reshape(N, 8, F, B)
    sizes = rng.permutation(np.array([8, 24, 64, 128, 256, 512, B, B]))[:, None]
    return x, q, pf, mb, fills(rng), backs(rng, points(rng, B)), starts(rng, sizes)
def pack(x, q, pf, mb, bd, ip, st):
    return {"xn": x.reshape(N, 128, B).astype(np.float32).astype(BF), "qr": q.reshape(N, 128, R).astype(np.float32).astype(BF),
            "pf": pf.reshape(N, 8 * F, B).astype(np.int32), "mb": mb.reshape(N, 8 * F, B).astype(np.int32), "bd": bd.reshape(N, 8 * F, B).astype(np.int32),
            "ip": ip.astype(np.int32), "st": np.stack([gtable(a) for a in st])}
def setup_inputs(rng):
    return pack(*parts(rng))
def setup_inputs_spread(rng):
    def uneven(shape):
        return np.minimum((B * rng.random(shape) ** 3).astype(np.int64), B - 1)
    x = np.minimum((np.exp2(8 * rng.random((N, 8, 1, B))) * rng.random((N, 8, 16, B))).astype(np.int64), 255)
    q = np.minimum((np.exp2(8 * rng.random((N, 8, 1, R))) * rng.random((N, 8, 16, R))).astype(np.int64), 255)
    return pack(x, q, uneven((N, 8, F, B)), B - 1 - uneven((N, 8, F, B)), fills(rng), backs(rng, uneven((N, 8, B))), uneven((N, 8, R)))
def setup_inputs_ends(rng):
    h = B // 2; lo = np.array([2, B - 3, 4, 0]); hi = np.array([B - 2, 1, B - 4, B - 1])
    def near(shape):
        return np.where(rng.random(shape) < 0.74, (B - 1) * rng.integers(0, 2, shape), rng.integers(3, h, shape))
    def ends(n):
        k = rng.integers(0, 4, (N, 8, 1, n)); m = 255 * rng.integers(0, 2, (N, 8, 16, n))
        return np.where(k == 0, 0, np.where(k == 1, 255, m))
    x = ends(B); q = ends(R); x[..., lo] = 0; x[..., hi] = 255
    pf = near((N, 8, F, B)); pf[..., 0] = lo[:F]; pf[..., B - 1] = hi[:F]; mb = near((N, 8, F, B))
    bd = np.where(rng.random((N, 8, F, B)) < 0.8, 7 * rng.integers(0, 2, (N, 8, F, B)), rng.integers(0, 8, (N, 8, F, B)))
    bd[:, 7, :, 0] = 7; bd[:, 7, :, B - 1] = 7
    v = near((N, 8, B)); ip = 4 * v + np.where(v == 0, 0, np.where(v == B - 1, F - 1, rng.integers(0, F, v.shape)))
    st = near((N, 8, R)); st[..., R - 1] = B - 1; q[..., R - 1] = 0; st[..., R - 2] = 0; q[..., R - 2] = 255
    ids = h + np.arange((S + 2) * 4).reshape(S + 2, 4)
    st[..., L - 4:L] = ids[0]
    for s in range(S):
        pf[..., ids[s]] = ids[s + 1]; bd[..., ids[s]] = 7
    bd[..., ids[S - 1]] = 6; bd[..., ids[S + 1]] = 6; ip[..., ids[S - 1]] = 4 * ids[S + 1] + F - 1
    if ST == 2 and RO >= 3 and S <= 3:
        n0 = h + (S + 2) * 4
        a0, a1, w1, w2, w3, y1, b0, b1, y2, z1, e0, e1 = (n0 + np.arange(12)).tolist()
        x[..., n0:n0 + 12] = 0; x[:, :, :2, n0:n0 + 12] = 4; x[:, :, 1, y2] = 3; x[:, :, 8:, b1] = 255; x[:, :, 8:, y1] = 64
        bd[..., n0:n0 + 12] = 7; bd[..., w2] = 6; bd[..., y2] = 6
        for i, j in ((a0, a1), (a1, w1), (w1, w2), (w2, w3), (b0, b1), (b1, w1), (e0, e1), (e1, y2), (y2, z1)):
            pf[..., i] = j
        pf[:, :, 0, w1] = y1; mb[..., w2] = y2
        ip[..., w2] = 4 * w1 + 2; ip[..., w1] = 4 * z1 + 1; ip[..., y2] = 4 * z1 + F - 1
        q[..., L - 9:L - 4] = 0; q[:, :, :2, L - 9:L - 4] = 4; q[:, :, 8:, L - 8] = 255; q[:, :, 0, L - 6] = 3; q[:, :, 1, L - 5] = 3
        st[..., L - 9:L - 4] = np.array([e0, b0, a0, a1, a1] if S == 3 else [e1, b1, a1, w1, w1])
    return pack(x, q, pf, mb, bd, ip, st)
def setup_inputs_corners(rng):
    x, q, pf, mb, bd, ip, st = parts(rng)
    cnt = rng.choice(np.array([0, 1, CAP - 1, CAP, CAP + 1, L]), (N, 8))
    cnt[0] = (CAP, CAP + 1, L, CAP - 1, 1, 0, CAP, L); cnt[1] = (CAP, L, CAP, CAP + 1, CAP, L, 0, CAP)
    cnt[(0 - (RO - 1) % (N - 1)) % N, 5] = CAP
    c = rng.integers(0, 5, (N, 8, F, B)); own = np.arange(B)
    pf = np.where(c == 0, 0, np.where(c == 1, B - 1, np.where(c == 2, own, pf)))
    st[..., R - 1] = B - 1; st[..., R - 2] = 0
    for r in range(N):
        for g in range(8):
            n = int(cnt[r, g]); od = rng.permutation(B); ids = od[:(S + 2) * L].reshape(S + 2, L)
            hit = np.sort(rng.permutation(L)[:n]); low = np.searchsorted(hit, np.arange(L)) - 1
            kind = rng.integers(0, 4, L)
            if ST == 1:
                kind = np.where(kind == 1, 0, np.where(kind == 3, 2, kind))
            kind[low < 0] = 0; kind[hit] = 4
            above = hit[np.maximum(low, 0)] if n else np.zeros(L, np.int64)
            a = st[r, g]; p = pf[r, g]; b = bd[r, g]
            a[:L] = np.where(kind == 2, ids[0][above], ids[0])
            for s in range(S):
                p[:, ids[s]] = ids[s + 1]; b[:, ids[s]] = 7
            b[:, ids[S - 1][(kind == 1) | (kind >= 3)]] = 6
            b[:, ids[S + 1]] = np.where(kind == 4, 5, 7)
            k = rng.integers(0, F, L)
            e = np.where((kind == 4) & (rng.random(L) < 0.2), 4 * ids[S - 1] + k, 4 * ids[S + 1] + k)
            e = np.where(kind == 3, e[above], e)
            ip[r, g][ids[S - 1]] = e
            if r == 1 and g == 5:
                alt = od[(S + 2) * L:(2 * S + 3) * L].reshape(S + 1, L); both = od[:(2 * S + 3) * L]
                xv = x[r, g]; qv = q[r, g]
                xv[:, both] = 0; xv[0, both] = 3; qv[:, :L] = 0; qv[0, :L] = 4
                mb[r, g][:, ids[0]] = alt[0]; b[:, ids[0]] = rng.integers(1, 4, (F, L))
                for s in range(S - 1):
                    p[:, alt[s]] = alt[s + 1]
                b[:, alt.reshape(-1)] = 7; ip[r, g][alt[S - 2]] = 4 * alt[S] + k
    return pack(x, q, pf, mb, bd, ip, st)
def setup_inputs_ties(rng):
    x, q, pf, mb, bd, ip, st = parts(rng)
    col = rng.choice(np.array([0, 1, 2, 255]), (N, 8, 16, 6))
    x = np.take_along_axis(col, rng.integers(0, 6, (N, 8, 1, B)), 3); q = np.take_along_axis(col, rng.integers(0, 6, (N, 8, 1, R)), 3)
    q[..., ::3] = np.minimum(q[..., ::3] + rng.integers(0, 2, q[..., ::3].shape), 255)
    m = rng.random((N, 8, B)) < 0.5
    pf[:, :, 1] = np.where(m, pf[:, :, 0], pf[:, :, 1]); mb[:, :, 2] = np.where(m, pf[:, :, 1], mb[:, :, 2])
    bd = np.where(bd == 7, 7, rng.integers(0, 4, bd.shape))
    st = starts(rng, rng.permutation(np.array([2, 3, 5, 9, 17, 33, 200, B]))[:, None])
    return pack(x, q, pf, mb, bd, ip, st)
def check_inputs(d):
    bad = []
    for k, lo, hi in (("xn", 0, 255), ("qr", 0, 255), ("pf", 0, B - 1), ("mb", 0, B - 1), ("bd", 0, 7), ("ip", 0, 4 * (B - 1) + F - 1), ("st", 0, B - 1)):
        a = np.asarray(d[k]).astype(np.float64)
        if not (np.min(a) >= lo and np.max(a) <= hi): bad.append("range of " + k)
        elif np.any(a != np.floor(a)): bad.append("whole numbers of " + k)
    if np.any((np.asarray(d["ip"]).astype(np.int64) & 3) >= F): bad.append("field of ip")
    return bad
def reference(xn, qr, pf, mb, bd, ip, st):
    X = np.zeros((N, 8, 16, W), np.int64); P = np.zeros((N, 8, F, W), np.int64); M = np.zeros((N, 8, F, W), np.int64)
    D = np.full((N, 8, F, W), 7, np.int64); I = np.zeros((N, 8, W), np.int64)
    X[..., :B] = xn.astype(np.float32).astype(np.int64).reshape(N, 8, 16, B); q = qr.astype(np.float32).astype(np.int64).reshape(N, 8, 16, R)
    P[..., :B] = pf.reshape(N, 8, F, B); M[..., :B] = mb.reshape(N, 8, F, B); D[..., :B] = bd.reshape(N, 8, F, B); I[..., :B] = ip
    start = np.stack([gentries(a) for a in st]).astype(np.int64)
    for t in range(RO):
        tau = np.add.reduce(q, axis=2) & 3; v = start
        for s in range(S):
            i = v[:, :, None, :]
            to = np.where(np.take_along_axis(D, i, 3) <= tau[:, :, None, :], np.take_along_axis(M, i, 3), np.take_along_axis(P, i, 3))
            xt = np.take_along_axis(X, to.reshape(N, 8, 1, F * R), 3).reshape(N, 8, 16, F, R)
            score = np.add.reduce(np.abs(xt - q[:, :, :, None, :]), axis=2)
            k = np.argmin(score, axis=2)
            u = v; v = np.take_along_axis(to, k[:, :, None, :], 2)[:, :, 0]
            q = (q + np.take_along_axis(X, v[:, :, None, :], 3)) >> 1
        base = B + (1 + ST) * L * t; left = {}
        for r in range(N):
            for g in range(8):
                x_, p_, m_, d_, i_ = X[r, g], P[r, g], M[r, g], D[r, g], I[r, g]
                wu, wk, vv, ql = u[r, g, :L], k[r, g, :L], v[r, g, :L], q[r, g][:, :L]
                lane = np.arange(L); wm = base + lane; e = 4 * wu + wk
                p_[:, wm] = p_[:, vv]; m_[:, wm] = m_[:, vv]; d_[:, wm] = d_[:, vv]; x_[:, wm] = ql; i_[wm] = e
                c, first = np.unique(vv, return_index=True)
                x_[:, c] = (x_[:, c] + ql[:, first]) >> 1; i_[c] = e[first]
                for z in range(1, ST + 1):
                    f = np.sort(np.unique(wu, return_index=True)[1])
                    lane, wu, wk, wm = lane[f], wu[f], wk[f], wm[f]
                    full = d_[wk, wu] != 7; o = ~full
                    m_[wk[o], wu[o]] = wm[o]; d_[wk[o], wu[o]] = t + 1
                    lane, wu, wk, wm = lane[full], wu[full], wk[full], wm[full]
                    c = base + L * z + lane
                    y = np.where(d_[:, wu] != 7, m_[:, wu], p_[:, wu]); y[wk, np.arange(len(wu))] = wm
                    x_[:, c] = x_[:, wu]; p_[:, c] = y; m_[:, c] = 0; d_[:, c] = 7
                    e = i_[wu]; i_[c] = e
                    wu, wk, wm = e >> 2, e & 3, c
                left[r, g] = lane[:CAP]
        old = q.copy()
        for r in range(N):
            s = (r - 1 - t % (N - 1)) % N
            for g in range(8):
                h = min(len(left[r, g]), len(left[s, g]))
                q[r, g][:, left[r, g][:h]] = old[s, g][:, left[s, g][:h]]
    return {"yx": X.reshape(N, 128, W).astype(np.float32).astype(BF), "yq": q.reshape(N, 128, R).astype(np.float32).astype(BF),
            "yp": P.reshape(N, 8 * F, W).astype(np.float32), "ym": M.reshape(N, 8 * F, W).astype(np.float32)}

import numpy as np
from concourse.mybir import AluOpType as ALU, ActivationFunctionType as AF

S_ = np.s_
B, W, NR, L, CAP = 1472, 2240, 384, 128, 48
PAD = 128
OFF = PAD + 16
TW = OFF + W
W1 = B + 3 * L
MAGIC = float(3 << 22)
BIGZ = 4096.0
TRI = 576
BLOCKS = (("w", 0, 128), ("n", 128, 384))
F32, BF, F16, I32, U16 = "float32", "bfloat16", "float16", "int32", "uint16"
OPT = {"diff": {"w": "vva", "n": "a"}, "round": {"w": "a", "n": "a", "x": "a"}, "sum": "tvvvvvvttttt", "meta": "vv", "m0": 1000,
       "tau": "t", "last": "v"}

SCRATCH = {}


def _buf(name, shape, dt, where="sbuf"):
    SCRATCH[name] = (where, [128] + list(shape), dt)


for _n, _s, _d in (
        ("X0", [B], BF), ("X1", [TW], BF), ("X2", [TW], BF), ("M0", [B], I32), ("M1", [TW], F32), ("M2", [TW], F32),
        ("Z", [OFF + W1], I32), ("IOTA", [W1 + L], F32), ("STI", [24], I32), ("LST", [24], U16),
        ("J", [4, 32], F32), ("G8", [128], F32), ("P16", [128], F32), ("JR", [128], F32), ("WC", [8], F32),
        ("KI", [4], I32), ("COL", [16], F32), ("LM", [2, 4, 32], F16), ("LT", [3, 4, 32], BF), ("LMF", [2, 4, 32], F32), ("GF", [256], F32), ("QH", [7 * 256], F16), ("LW0", [512], BF), ("ZB", [256], BF),
        ("LW", [16, 128], BF), ("E8", [8], BF), ("LS", [2, 128], BF), ("LC", [128], BF), ("CK", [48], BF),
        ("HI", [128], BF), ("IB", [2, 128], BF), ("CN", [256], BF), ("IF", [2, 128], F32), ("ONEF", [128], F32),
        ("BQ", [128], BF), ("CT", [256], BF), ("BO", [128], BF), ("LR", [2, 128], BF),
        ("MK", [128], F32), ("RS16", [128], F32), ("RS3", [48], F32), ("JROW", [128], F32), ("RST", [TRI], BF),
        ("LE", [2], U16), ("CW", [10, 8], F32), ("SD0", [5 * 16], F32), ("SD1", [3 * 16], F32), ("SDO", [3 * 16], F32),
        ("JD", [8], F32), ("KT", [8], F32), ("KT2", [8], F32), ("KD", [8], F32), ("KA1", [8], F32), ("KA2", [8], F32),
        ("SHD", [128], F32), ("SHM", [2, 128], F32), ("BC", [8], F32), ("MROW", [4, 128], F32), ("VROW", [4, 128], F32),
        ("KROW", [3, 128], F32), ("ABS", [3 * TRI], BF), ("SCN", [3 * (TRI + 16)], BF), ("SM", [32, 8], F32),
        ("SI", [6, 8], I32), ("LP", [12 * 8], U16), ("ROW", [14 * 128], F32), ("XMIX", [128], BF), ("WD", [128], BF),
        ("TD", [8, 32], F32), ("K3", [3 * 24], F32), ("LEFT", [8], BF), ("SC", [10], BF),
        ("CB", [2 * 384], BF), ("QIN0", [128], BF), ("QIN1", [128], BF), ("LIN0", [8], U16), ("LIN1", [8], U16),
        ("LOUT0", [8], U16), ("LOUT1", [8], U16)):
    _buf(_n, _s, _d)
for _b, _lo, _hi in BLOCKS:
    _r = _hi - _lo
    _c = _r // 16
    for _n, _s, _d in (("Q", [8 * _r], BF), ("G", [_r], F16), ("TR", [_c, 32], F32), ("A", [_c, 6], F32),
                       ("T", [3 * _c], F32), ("LK", [3 * _c], U16), ("D", [3 * _r], BF), ("AD", [_c, 3, 16], BF),
                       ("KK", [3 * 3 * _c], F32), ("V", [3, _c], F32), ("LV", [3 * _c], U16),
                       ("XV", [_r], BF), ("FL", [_r], F32), ("FR", [_r], BF), ("FR2", [_c, 2, 16], BF)):
        _buf(_n + _b, _s, _d)
    _buf("pm" + _b, [16, 2, 16], F32, "psum")
    _buf("ps" + _b, [512], F32, "psum")
    _buf("pq" + _b, [8, 4, 16], F32, "psum")
_buf("pa", [16, 2, 16], F32, "psum")
_buf("px", [8, 4, 16], F32, "psum")

NDMA = 40
SEMAPHORES = ["v", "a", "t", "g", "sent", "aq0", "al0", "aq1", "al1"] + ["d%d" % _i for _i in range(NDMA)]

CYC, FIX, WAKE, GATH, SCAT, PEC = 1.0, 60.0, 70.0, 1.55, 3.5, 0.55
LOOK, TURNS = 40.0, 12


def span(ap):
    name, idx = ap[0], ap[1]
    if name not in SCRATCH:
        return name, 0, 1 << 20, 0
    shape = SCRATCH[name][1][1:]
    idx = idx if isinstance(idx, tuple) else (idx,)
    flat = np.arange(int(np.prod(shape))).reshape(shape)[idx[1:]].ravel()
    if SCRATCH[name][0] == "psum":
        return name, 0, 512, int(flat.size)
    return name, int(flat.min()), int(flat.max()) + 1, int(flat.size)


def a(name, idx=S_[:]):
    return (name, idx)


def cols(name, lo, hi, step=None):
    return (name, S_[:, lo:hi:step] if step else S_[:, lo:hi])


def ind(win, off):
    return (win[0], win[1], off)


def two_bytes(*aps):
    return all(SCRATCH[x[0]][2] in (BF, F16, U16) for x in aps)


def build(rank, core, T, topo, g):
    ops = []

    def real(x):
        if not isinstance(x, tuple):
            return x
        r = T[x[0]][x[1]]
        return r.indirect(real(x[2])) if len(x) == 3 else r

    def add(eng, fn, outs, ins, busy, lat=0.0, dma=0, sem=None, loose=False):
        rd, wr = [], []
        for x in ins:
            if isinstance(x, tuple):
                rd.append(span(x)[:3])
                if len(x) == 3:
                    rd.append(span(x[2])[:3])
        for x in outs:
            wr.append(span(x)[:3])
            if len(x) == 3:
                rd.append(span(x[2])[:3])
        ops.append({"eng": eng, "fn": fn, "rd": rd, "wr": wr, "busy": busy, "lat": lat, "dma": dma, "sem": sem})

    def count(out, in0):
        if len(in0) == 3:
            return span(out)[3], GATH
        if len(out) == 3:
            return span(in0)[3], SCAT
        return span(in0)[3], None

    def vcost(out, in0, per):
        n, c = count(out, in0)
        return 50 + c * n * CYC if c else max(FIX, per * n * CYC)

    def cp(out, in_):
        add("v", lambda: g.vector.tensor_copy(real(out), real(in_)), [out], [in_],
            vcost(out, in_, 0.5 if two_bytes(out, in_) else 1))

    def tt(out, x, y, op):
        ps = SCRATCH[x[0]][0] == "psum" or SCRATCH[y[0]][0] == "psum"
        add("v", lambda: g.vector.tensor_tensor(real(out), real(x), real(y), op), [out], [x, y], vcost(out, x, 1 if ps else 2))

    def ts(out, x, s1, op0, s2=None, op1=None):
        if op1 is None:
            fn = lambda: g.vector.tensor_scalar(real(out), real(x), real(s1), None, op0)
        else:
            fn = lambda: g.vector.tensor_scalar(real(out), real(x), real(s1), real(s2), op0, op1)
        add("v", fn, [out], [x, s1, s2], vcost(out, x, 0.5 if two_bytes(out, x) else 1))

    def ms(out, val):
        add("v", lambda: g.vector.memset(real(out), val), [out], [], vcost(out, out, 0.5 if two_bytes(out) else 1))

    def scan(out, d0, d1, init, op0, op1):
        add("v", lambda: g.vector.tensor_tensor_scan(real(out), real(d0), real(d1), init, op0, op1), [out], [d0, d1],
            vcost(out, d1, 0.5 if two_bytes(out, d0, d1) else 1))

    def tr(out, in_):
        add("v", lambda: g.vector.transpose(real(out), real(in_)), [out], [in_], vcost(out, in_, 1))

    def act(out, in_, func=AF.Identity, bias=0.0, scale=1.0):
        n, c = count(out, in_)
        add("a", lambda: g.scalar.activation(real(out), real(in_), func, bias=real(bias), scale=real(scale)),
            [out], [in_, bias, scale], 65 + c * n * CYC if c else max(FIX, n * CYC) + 10)

    def mm(out, lhs, rhs, start, stop):
        n = span(rhs)[3]
        add("t", lambda: g.tensor.matmul(real(out), real(lhs), real(rhs), start, stop), [out], [lhs, rhs],
            max(64, n) * PEC * (4 if SCRATCH[lhs[0]][2] == F32 else 1), lat=40.0)

    def iota(out, pat, base, cm):
        if SCRATCH[out[0]][2] == I32:
            fn = lambda: g.iota(real(out), pat, base, cm)
        else:
            fn = lambda: g.iota(real(out), pat, base, cm, allow_small_or_imprecise_dtypes=True)
        add("g", fn, [out], [], 130 + 2 * span(out)[3] * CYC)

    def fill(out, val):
        iota(out, [[0, span(out)[3]]], val, 0)

    def sel(out, in_, pat, op, val, base, cm):
        add("g", lambda: g.affine_select(real(out), real(in_), pat, op, val, base, cm), [out], [in_],
            170 + 2 * span(out)[3] * CYC)

    def dma(q, pairs, nbytes, after=()):
        eng = {"s": g.sync, "a": g.scalar}[q]
        add(q, [(lambda o=o, i=i: eng.dma_start(real(o), real(i))) for o, i in pairs],
            [o for o, i in pairs], [i for o, i in pairs] + list(after), 60.0 * len(pairs), lat=1700 + nbytes / 180.0, dma=len(pairs))

    def send(t, what, dst_buf, src):
        dst = T.cores[(rank + 1 + t % 3) % len(T.cores)]
        frm = T.cores[(rank - 1 - t % 3) % len(T.cores)]
        rid, pid = topo.addr(dst, core)
        mask = topo.mask(core, dst)
        sem = "a%s%d" % (what, t)
        add("g", lambda: g.remote_dma(real(dst_buf), real(src), T.sem[sem], T.sem.sent, pid, rid, mask),
            [a("flight" + sem)], [src], 300.0, lat=2000.0, sem=("sent", len(topo.engines(core, dst))))
        add("x", None, [dst_buf], [a("flight" + sem)], 0.0, sem=(sem, len(topo.engines(frm, core))))

    ms(cols("M0", 0, OPT["m0"]), 0)
    if OPT["m0"] < B:
        fill(cols("M0", OPT["m0"], B), 0)
    dma("a", [(a("STI"), a("st"))], 12e3)
    dma("a", [(cols("Q" + b, 0, hi - lo), a("qr", S_[:, lo:hi])) for b, lo, hi in BLOCKS], 98e3)
    dma("a", [(a("X0"), a("xn"))], 500e3)
    dma("s", [(a("M0", S_[3 * i + k::16, :]), a(src, S_[k::3, :])) for i, src in enumerate(("pf", "mb", "bd")) for k in range(3)], 500e3)
    dma("s", [(cols("X1", OFF, OFF + B), a("xn"))], 400e3, after=[a("M0"), a("X0")])
    dma("s", [(a("Z", S_[p::16, OFF:OFF + B]), a("ip")) for p in range(16)], 1100e3, after=[a("M0"), a("X0")])

    col = lambda i: cols("COL", i, i + 1)
    RHO, GC, SUB, ISP, ISM, GE6, C7, ODD, ME, MO, TA, TB = (col(i) for i in (0, 1, 4, 5, 6, 7, 8, 2, 9, 3, 10, 11))
    cw = lambda i: a("CW", S_[:, i, :])
    WI, CK1, CK0, CD1, CD0, C128, C256 = (cw(i) for i in range(7))
    CDEAD = [cw(7), cw(8)]
    KM = [[-1, 128]]
    iota(cols("KI", 0, 1), [[1, 1]], 0, 1)
    iota(a("J"), KM, 0, 1)
    iota(a("G8"), [[1, 8], [0, 16]], 0, 0)
    iota(a("P16"), [[0, 8], [1, 16]], 0, 0)
    iota(a("JR"), [[1, 128]], 0, 0)
    iota(a("WC"), [[16, 8]], 0, 0)
    ts(cols("KI", 3, 4), cols("KI", 0, 1), 4, ALU.arith_shift_right, 1, ALU.bitwise_and)
    ts(cols("KI", 2, 3), cols("KI", 0, 1), 1, ALU.bitwise_and)
    ts(cols("KI", 1, 2), cols("KI", 0, 1), 4, ALU.arith_shift_right)
    ts(cols("KI", 0, 1), cols("KI", 0, 1), 15, ALU.bitwise_and)
    cp(cols("COL", 0, 4), a("KI"))
    ts(ISM, RHO, 6.0, ALU.is_lt)
    ts(SUB, ISM, 1022.0, ALU.mult, 2.0, ALU.add)
    ts(ME, MO, -1.0, ALU.mult, 1.0, ALU.add)
    cp(a("LST"), a("STI"))
    ms(a("LM"), 0.0)
    ms(a("LT"), 0.0)
    for h in range(2):
        for r0, i0, w in ((0, 3, 1.0), (3, 0, 1.0), (6, 6, -BIGZ), (9, 6, BIGZ), (12, 6, 1.0)):
            ts(a("LM", S_[:, h, :, r0:r0 + 3]), a("J", S_[:, :, r0:r0 + 3]), float(16 * h + i0 - r0), ALU.is_equal, w, ALU.mult)
    ts(a("BO"), a("G8"), GC, ALU.is_equal)
    for h in range(2):
        for r0, w in ((6, 4 * BIGZ), (9, -4 * BIGZ)):
            ts(a("LT", S_[:, h, :, r0:r0 + 3]), a("J", S_[:, :, r0:r0 + 3]), float(16 * h - r0), ALU.is_equal, w, ALU.mult)
    tt(a("LT", S_[:, 2, :, 6:12]), a("LT", S_[:, 0, :, 6:12]), a("LT", S_[:, 1, :, 6:12]), ALU.add)
    if "a" in OPT["meta"]:
        cp(a("LMF"), a("LM"))
        act(col(12), SUB, scale=-1.0)
    ms(a("LW"), 0.0)
    ts(a("E8"), cols("G8", 0, 128, 16), GC, ALU.is_equal, 8192.0, ALU.mult)
    for p in range(16):
        act(a("LW", S_[:, p, p::16]), a("E8"), AF.Copy)
    fill(a("LS"), 0)
    for h in range(2):
        act(a("LS", S_[:, h, 0::32]), cols("E8", h, 8, 2), AF.Copy)
    fill(a("LC"), 1)
    ms(a("CK", S_[0:64, :]), -float(1 << 18))
    for k in range(3):
        ms(a("CK", S_[64:128, k::3]), 32.0 * (k + 4))
    ts(a("HI"), a("J"), 0.0, ALU.is_equal, 0.5, ALU.mult)
    act(a("IB", S_[:, 0, :]), a("HI"), scale=2.0)
    act(a("IB", S_[:, 1, :]), a("HI"), scale=-2.0)
    act(a("IF", S_[:, 0, :]), a("HI"), scale=2.0)
    act(a("IF", S_[:, 1, :]), a("HI"), scale=-2.0)
    ms(a("CN"), -0.5)
    act(a("BQ"), a("BO"), scale=0.25)
    ms(a("CT"), -3.0 / 32)
    ms(a("RS3"), 0.0)
    ms(cols("RS3", 0, 48, 3), 1e9)
    fill(a("ZB"), 0)
    ms(a("LW0"), 0.0)
    fill(a("ONEF"), 1)
    sel(a("LR", S_[:, 0, :]), a("BO"), [[1, 128]], ALU.is_gt, 0.0, 0, -1)
    sel(a("LR", S_[:, 1, :]), a("LR", S_[:, 0, :]), KM, ALU.not_equal, -256.0, 0, 1)
    sel(a("RS16"), a("ONEF"), [[0, 8], [1, 16]], ALU.not_equal, 0.0, 0, 0)
    sel(a("SHD"), a("ONEF"), KM, ALU.is_equal, 0.0, -6, 1)
    sel(a("SHM", S_[:, 0, :]), a("ONEF"), KM, ALU.is_equal, 0.0, -3, 1)
    sel(a("SHM", S_[:, 1, :]), a("SHM", S_[:, 0, :]), KM, ALU.not_equal, -1.0, 0, 1)
    ts(a("MK"), a("P16"), RHO, ALU.is_equal)
    act(a("JROW"), a("JR"), scale=1.0 / 256)
    act(WI, a("WC"), bias=RHO)
    act(CK1, WI, scale=-1.0 / 256, bias=0.25 - 1024)
    act(CK0, WI, scale=-1.0 / 256, bias=0.25)
    act(C128, WI, bias=128.0)
    act(C256, WI, bias=256.0)
    for t in range(2):
        act(CDEAD[t], WI, scale=4.0, bias=16384.0 + 4 * (B + 3 * L * t))
    fill(a("SD0"), 0)
    for i in range(3):
        act(cols("SD1", 16 * i + 1, 16 * i + 16, 2), WI, AF.Copy)
    fill(a("RST"), 0)
    for c in range(8):
        fill(cols("RST", 8 * c * (c + 1), 8 * c * (c + 1) + 1), 1 << 14)
    for i in range(3):
        fill(cols("SCN", (TRI + 16) * i + TRI, (TRI + 16) * (i + 1)), 0)
    ts(TA, RHO, 3.0, ALU.add, 2.0, ALU.mult)
    ts(TB, RHO, 1.0, ALU.add, TA, ALU.mult)
    ts(TA, TB, -1.0 - TRI, ALU.add, ODD, ALU.mult)
    ts(cols("LE", 0, 1), TA, float(TRI), ALU.add)
    ts(ISP, RHO, 3.0, ALU.is_lt)
    ts(GE6, RHO, 6.0, ALU.is_ge)
    act(C7, GE6, scale=7.0)
    ts(a("JD"), cols("JR", 0, 8), RHO, ALU.subtract)
    ts(a("KD"), a("JD"), -6.0, ALU.is_equal)
    ts(a("KT2"), a("JD"), -3.0, ALU.is_equal)
    tt(a("KT"), a("KT2"), a("KD"), ALU.add)
    ts(a("KA2"), a("JD"), 0.0, ALU.is_equal, GE6, ALU.max)
    fill(cols("KA1", 3, 8), 0)
    ts(cols("KA1", 0, 3), cols("JD", 0, 3), 0.0, ALU.not_equal, ISP, ALU.mult)
    for i in range(4):
        t, z = divmod(i, 2)
        mb = float(B + 3 * L * t + L * z)
        act(cols("BC", i, i + 1), ISP, scale=mb, bias=C7)
        act(a("MROW", S_[:, i, :]), a("JR"), bias=cols("BC", i, i + 1), scale=ISP)
        act(cols("BC", 4 + i, 5 + i), ISM, scale=mb - (t + 1), bias=float(t + 1))
        act(a("VROW", S_[:, i, :]), a("JR"), bias=cols("BC", 4 + i, 5 + i), scale=ISM)
    fill(cols("SC", 0, 1), 16)
    fill(a("CB"), 0)
    fill(cols("X1", PAD, OFF), 0)
    fill(cols("X2", PAD, OFF), 0)
    fill(cols("Z", OFF + B + 2 * L, OFF + W1), 0)
    iota(cols("IOTA", 0, 496), [[1, 496]], 0, 0)
    for lo in range(496, W1 + L, 496):
        act(cols("IOTA", lo, lo + 496), cols("IOTA", 0, 496), bias=float(lo))
    for lo in range(0, B, 368):
        sel(cols("M1", OFF + lo, OFF + lo + 368), cols("M0", lo, lo + 368), [[0, 368]], ALU.is_ge, 0.0, 0, 0)

    def halve(out, x, y, pq, n, how, tmp):
        if how == "v":
            mm(pq, a("HI"), cols("CN", 0, n), True, False)
        mm(pq, a("HI"), x, how != "v", False)
        mm(pq, a("HI"), y, False, True)
        if how == "v":
            ts(out, pq, MAGIC, ALU.add, MAGIC, ALU.subtract)
        elif how == "h":
            act(out, pq, bias=512 - 0.25)
        else:
            act(tmp, pq, scale=0.999, bias=MAGIC)
            act(out, tmp, bias=-MAGIC)

    def reads(b, lo, hi, t, X, M):
        R = hi - lo
        C = R // 16
        high = OPT["round"][b] == "h"
        Q = lambda i: cols("QH" if high and i else "Q" + b, i * R, (i + 1) * R)
        q0 = 4 * t if b == "w" else 3 * t
        pq, pm, ps = a("pq" + b, S_[:, 0:R // 64]), "pm" + b, cols("ps" + b, 0, 3 * C)
        kk = lambda i: cols("KK" + b, 3 * C * i, 3 * C * (i + 1))
        mm(pq, a("BQ"), cols("CT", 0, R), True, False)
        mm(pq, a("BQ"), Q(q0), False, True)
        ts(a("FL" + b), pq, MAGIC, ALU.add, MAGIC, ALU.subtract)
        tt(a("FR" + b), pq, a("FL" + b), ALU.subtract)
        twice = b == "n" and OPT["tau"] == "a"
        for h in range(2 if twice else 0):
            act(a("FR2" + b, S_[:, :, h, :]), a("FR" + b), scale=(ME, MO)[h])
        lv = cols("LST", lo // 16, hi // 16)
        for s in range(3):
            q = Q(q0 + s)
            node = ("LM", "G" + b)
            if b == "n" and OPT["meta"][t] == "a":
                node = ("LMF", "GF")
                act(a("GF"), ind(M, lv), bias=col(12))
            else:
                ts(a("G" + b), ind(M, lv), SUB, ALU.subtract)
            if twice:
                mm(a(pm, S_[:, 0:C]), a("LT", S_[:, 2]), a("FR2" + b), True, False)
                terms = (node,)
            else:
                mm(a(pm, S_[:, 0:C]), cols("ZB", 0, 128), cols("LW0", 0, 2 * R), True, False)
                terms = (node, ("LT", "FR" + b)) if s == 0 else (("LT", "FR" + b), node)
            for i, (m, x) in enumerate(terms):
                for h in range(2):
                    mm(a(pm, S_[:, 0:C, h, :]), a(m, S_[:, h]), a(x), False, i == len(terms) - 1 and h == 1)
            tr(a("TR" + b), a(pm, S_[:, 0:C]))
            tt(a("A" + b), a("TR" + b, S_[:, :, 0:6]), a("TR" + b, S_[:, :, 6:12]), ALU.min)
            tt(a("T" + b), a("A" + b, S_[:, :, 0:3]), a("A" + b, S_[:, :, 3:6]), ALU.max)
            mm(ps, a("LC"), cols("CK", 0, 3 * C), True, False)
            if OPT["diff"][b] != "a":
                for k in (2, 0, 1):
                    lk, d = cols("LK" + b, k * C, (k + 1) * C), cols("D" + b, k * R, (k + 1) * R)
                    ts(lk, cols("T" + b, k, 3 * C, 3), 1024.0, ALU.add)
                    if OPT["diff"][b][k] == "v":
                        tt(d, ind(X, lk), q, ALU.subtract)
                    else:
                        mm(pq, a("IB", S_[:, 1, :]), q, True, False)
                        act(d, ind(X, lk), AF.Copy)
                        mm(pq, a("IB", S_[:, 0, :]), d, False, True)
                        d = pq
                    act(a("AD" + b, S_[:, :, k, :]), d, AF.Abs)
            else:
                ts(a("LK" + b), a("T" + b), 1024.0, ALU.add)
                for i in range(C // 8):
                    px, d = "px" if i == 0 else "pq" + b, cols("D" + b, 384 * i, 384 * (i + 1))
                    act(d, ind(X, cols("LK" + b, 24 * i, 24 * (i + 1))), AF.Copy)
                    mm(a(px, S_[:, :, 0:3, :]), a("IB", S_[:, 0, :]), d, True, False)
                    for k in range(3):
                        mm(a(px, S_[:, :, k, :]), a("IB", S_[:, 1, :]),
                           cols(q[0], (q0 + s) * R + 128 * i, (q0 + s) * R + 128 * (i + 1)), False, k == 2)
                    act(a("AD" + b, S_[:, 8 * i:8 * i + 8]), a(px, S_[:, :, 0:3, :]), AF.Abs, bias=1024.0 if q[0] == "QH" else 0.0)
            for p in range(16):
                mm(ps, a("LW", S_[:, p, :]), a("AD" + b, S_[:, :, :, p]), False, p == 15)
            tt(kk(0), ps, a("T" + b), ALU.add)
            scan(kk(1), cols("RS3", 0, 3 * C), ps, 0.0, ALU.add, ALU.min)
            scan(kk(2), cols("RS3", 0, 3 * C), kk(0), 0.0, ALU.add, ALU.min)
            tt(a("V" + b, S_[:, s, :]), cols("KK" + b, 6 * C + 2, 9 * C, 3), cols("KK" + b, 3 * C + 2, 6 * C, 3), ALU.subtract)
            lv = cols("LV" + b, s * C, (s + 1) * C)
            ts(lv, a("V" + b, S_[:, s, :]), 1024.0, ALU.add)
            act(a("XV" + b), ind(X, lv), AF.Copy)
            if high and q0 + s == 0:
                mm(pq, a("HI"), q, True, False)
                mm(pq, a("HI"), a("XV" + b), False, True)
                act(Q(1), pq, bias=1024 - 0.25)
            else:
                halve(Q(q0 + s + 1), q, a("XV" + b), pq, R, OPT["round"][b], a("FL" + b))
            if high and q0 + s == 5:
                act(cols("Q" + b, 6 * R, 7 * R), Q(6), bias=-1024.0) if OPT["last"] == "a" else ts(cols("Q" + b, 6 * R, 7 * R), Q(6), -1024.0, ALU.add)
            if b == "w" and s == 1:
                yield

    sm = lambda i: a("SM", S_[:, i, :])
    si = lambda i: a("SI", S_[:, i, :])
    lp = lambda i: cols("LP", 8 * i, 8 * i + 8)
    row = lambda i: cols("ROW", 128 * i, 128 * i + 128)
    flag = lambda i: cols("SD0", 16 * i + 1, 16 * i + 16, 2)
    diff = lambda i: cols("SD1", 16 * i, 16 * i + 16, 2)
    pa = lambda i: a("pa", S_[:, 4 * i:4 * i + 4])

    def lowest(i, lst, bias, slot):
        tt(a("KROW", S_[:, i, :]), ind(a("IOTA"), lst), a("JROW"), ALU.add)
        o, o2 = TRI * i, (TRI + 16) * i
        for c in range(7, -1, -1):
            act(cols("ABS", o + 8 * c * (c + 1), o + 8 * (c + 1) * (c + 2)), a("KROW", S_[:, i, 0:16 * (c + 1)]), AF.Abs,
                bias=a("SM", S_[:, bias, c:c + 1]))
        for lo, hi in ((240, TRI), (0, 240)):
            scan(cols("SCN", o2 + lo, o2 + hi), cols("RST", lo, hi), cols("ABS", o + lo, o + hi), 0.0, ALU.add, ALU.min)
        ts(cols("SD0", 16 * slot, 16 * slot + 16), ind(cols("SCN", o2, o2 + TRI + 16), cols("LE", 0, 1)), 0.25, ALU.is_ge)

    def choose(i, lst):
        s = lambda n: cols(n, 16 * i, 16 * i + 16)
        scan(s("SDO"), s("SD0"), s("SD1"), 0.0, ALU.mult, ALU.max)
        cp(lst, cols("SDO", 16 * i + 1, 16 * i + 16, 2))

    turn = [0]

    def combine(out, x, y, sign):
        turn[0] += 1
        if OPT["sum"][turn[0] - 1] == "v":
            tt(out, x, y, ALU.add if sign > 0 else ALU.subtract)
        else:
            mm(pa(3), a("IF", S_[:, 0, :]), x, True, False)
            mm(pa(3), a("IF", S_[:, 0 if sign > 0 else 1, :]), y, False, True)
            act(out, pa(3), AF.Copy)

    def fields(gr, y):
        mm(pa(0), a("SHD"), gr, True, True)
        mm(pa(1), a("SHM", S_[:, 1, :]), gr, True, True)
        act(row(9), pa(0), AF.Sign, scale=-1.0, bias=7.0)
        tt(row(12), pa(1), row(9), ALU.mult)
        combine(y, row(12), gr, 1)

    def copies(t, z, Xb, Mb, y, alive, k3, node16, i0):
        base = B + 3 * L * t
        c0 = OFF + base + L * z
        tt(sm(i0), k3, alive, ALU.mult)
        ts(lp(8), sm(i0), 3.0, ALU.add)
        tt(sm(i0 + 1), node16, alive, ALU.mult)
        cp(lp(9), sm(i0 + 1))
        tt(row(10), ind(a("KA1"), lp(8)), y, ALU.mult)
        tt(row(11), ind(a("KA2"), lp(8)), a("MROW", S_[:, 2 * t + z - 1, :]), ALU.mult)
        combine(cols(Mb, c0, c0 + L), row(10), row(11), 1)
        act(cols(Xb, c0, c0 + L), ind(cols(Xb, PAD, OFF + base), lp(9)), AF.Copy)

    def before_last(t, Mf):
        lu, u = cols("LVw", 8, 16), a("Vw", S_[:, 1, :])
        tt(sm(0), CK1, u, ALU.subtract)
        lowest(0, lu, 0, 3)
        act(row(0), ind(a("IOTA"), lu), scale=4.0)
        act(row(1), ind(Mf, lu), AF.Copy)
        combine(row(2), a("VROW", S_[:, 2 * t, :]), row(1), -1)
        fields(row(1), row(3))
        act(diff(1), u, bias=1024.0 + OFF)
        act(sm(3), u, bias=1024.0 + 16)

    def parts(t, Mf, Xb, Mb):
        base = B + 3 * L * t
        n0 = OFF + base
        lu, lv, v = cols("LVw", 8, 16), cols("LVw", 16, 24), a("Vw", S_[:, 2, :])
        q = cols("Qw", (4 * t + 3) * L, (4 * t + 4) * L)
        qin, lin, lout = a("QIN%d" % t), a("LIN%d" % t), a("LOUT%d" % t)
        cb = cols("CB", 384 * t, 384 * (t + 1))
        least = cols("KKw", 24 + 2, 48, 3)
        send(t, "q", qin, q)
        cp(si(0), least)
        ts(si(1), si(0), 11, ALU.arith_shift_right, 3, ALU.bitwise_and)
        cp(lp(0), si(1))
        ts(sm(4), si(1), -3.0, ALU.add)
        ts(cols("K3", 0, 24), a("TRw", S_[:, :, 12:15]), 5.0, ALU.not_equal)
        tt(cols("K3", 24, 48), cols("psw", 0, 24), cols("K3", 0, 24), ALU.add)
        scan(cols("K3", 48, 72), cols("RS3", 0, 24), cols("K3", 24, 48), 0.0, ALU.add, ALU.min)
        tt(sm(5), cols("K3", 50, 72, 3), least, ALU.subtract)
        tt(sm(6), sm(5), flag(3), ALU.mult)
        tt(flag(1), flag(3), sm(6), ALU.subtract)
        act(sm(7), sm(6), scale=-1.0, bias=1.0)
        tt(sm(8), sm(7), CDEAD[t], ALU.mult)
        tt(sm(10), CK1, v, ALU.subtract)
        act(diff(0), v, bias=1024.0 + OFF)
        lowest(1, lv, 10, 0)
        choose(0, lp(1))
        tt(row(4), ind(cols("JR", 0, 8), lp(0)), row(0), ALU.add)
        cp(ind(cols("Z", 0, n0), lp(1)), row(4))
        act(cols(Mb, n0, n0 + L), ind(Mf, lv), AF.Copy)
        act(cols(Xb, n0, n0 + L), q, AF.Copy)
        halve(a("XMIX"), a("XVw"), q, a("pqw", S_[:, 0:2]), L, OPT["round"]["x"], a("FLw"))
        cp(ind(cols(Xb, 0, n0), lp(1)), a("XMIX"))
        choose(1, lp(2))
        tt(row(5), ind(a("KT"), lp(0)), row(2), ALU.mult)
        tt(ind(cols(Mb, 0, n0), lp(2)), row(5), row(1), ALU.add)
        zwin = cols("Z", OFF, n0)
        tt(row(6), ind(zwin, lu), a("MK"), ALU.mult)
        scan(row(7), a("RS16"), row(6), 0.0, ALU.mult, ALU.add)
        tt(si(2), cols("ROW", 128 * 7 + 15, 128 * 8, 16), sm(8), ALU.max)
        ts(si(3), si(2), 16383, ALU.bitwise_and, 2, ALU.arith_shift_right)
        cp(lp(3), si(3))
        ts(si(4), si(2), 3, ALU.bitwise_and)
        cp(lp(4), si(4))
        tt(sm(12), CK0, si(3), ALU.subtract)
        act(row(8), ind(cols(Mb, OFF, n0 + L), lp(3)), AF.Copy)
        lowest(2, lp(3), 12, 4)
        mm(a("pa", S_[:, 0:8]), cols("ZB", 0, 128), a("ZB"), True, False)
        tt(a("WD"), ind(a("KD"), lp(4)), row(8), ALU.mult)
        for h in range(2):
            mm(a("pa", S_[:, 0:8, h, :]), a("LS", S_[:, h, :]), a("WD"), False, h == 1)
        tr(a("TD"), a("pa", S_[:, 0:8]))
        ts(sm(15), a("TD", S_[:, :, 0]), 7.0 * 8192, ALU.not_equal)
        tt(sm(16), sm(15), sm(6), ALU.mult)
        tt(a("LEFT"), sm(16), flag(4), ALU.mult)
        scan(cols("SC", 1, 9), cols("ONEF", 0, 8), a("LEFT"), 16.0, ALU.mult, ALU.add)
        pr = cols("psw", 32, 40)
        mm(pr, a("LR", S_[:, 1, :]), a("LEFT"), True, False)
        mm(pr, a("BO"), cols("SC", 0, 8), False, True)
        tt(sm(17), pr, C128, ALU.min)
        cp(lout, sm(17))
        send(t, "l", lin, lout)
        ts(sm(18), pr, float(CAP), ALU.is_ge, 1000.0, ALU.mult)
        tt(sm(19), pr, sm(18), ALU.max)
        tt(sm(20), sm(19), C256, ALU.min)
        cp(lp(5), sm(20))
        cp(ind(cb, lp(5)), q)
        copies(t, 1, Xb, Mb, row(3), sm(6), sm(4), sm(3), 21)
        if t == 0:
            cp(cols("Z", n0, n0 + L), row(4))
            cp(cols("Z", n0 + L, n0 + 2 * L), ind(zwin, lu))
        tt(sm(23), flag(4), sm(6), ALU.mult)
        tt(flag(2), sm(23), a("LEFT"), ALU.subtract)
        ts(diff(2), si(3), float(OFF), ALU.add)
        choose(2, lp(6))
        combine(row(13), a("VROW", S_[:, 2 * t + 1, :]), row(8), -1)
        tt(row(5), ind(a("KT"), lp(4)), row(13), ALU.mult)
        tt(ind(cols(Mb, 0, n0), lp(6)), row(5), row(8), ALU.add)
        fields(row(8), row(3))
        ts(sm(24), si(4), -3.0, ALU.add)
        act(sm(25), diff(2), bias=16.0 - OFF)
        copies(t, 2, Xb, Mb, row(3), a("LEFT"), sm(24), sm(25), 26)
        cp(ind(cb, lin), qin)
        cp(cols("Qw", (4 - 4 * t) * L, (5 - 4 * t) * L), ind(cb, lp(5)))

    def store(name, src, r0, lo, hi, q):
        dma(q, [(a(name, S_[k::3, lo:hi]), a(src, S_[r0 + k::16, OFF + lo:OFF + hi])) for k in range(3)], 96 * (hi - lo))

    for t in range(2):
        X = a("X0") if t == 0 else cols("X1", OFF, OFF + W1 - L)
        M = a("M0") if t == 0 else cols("M1", OFF, OFF + W1 - L)
        Mf = cols("M1", OFF, OFF + B + 2 * L * t)
        Xb, Mb = ("X1", "M1") if t == 0 else ("X2", "M2")
        for _ in reads("w", 0, 128, t, X, M):
            before_last(t, Mf)
        parts(t, Mf, Xb, Mb)
        for _ in reads("n", 128, 384, t, X, M):
            pass
        if t == 0:
            dma("s", [(cols("X2", OFF, OFF + W1), cols("X1", OFF, OFF + W1))], 480e3)
            dma("s", [(cols("M2", OFF, OFF + W1), cols("M1", OFF, OFF + W1))], 1400e3)
            store("yp", "M1", 0, 0, W1, "s")
    dma("s", [(a("yx", S_[:, 0:W1 + L]), cols("X2", OFF, OFF + W1 + L))], 510e3)
    store("ym", "M2", 3, 0, W1, "s")
    dma("s", [(a("yx", S_[:, W1 + L:W]), cols("X2", OFF + W1 + L, TW))], 66e3)
    store("yp", "M2", 0, W1, W, "s")
    store("ym", "M2", 3, W1, W, "s")
    dma("s", [(a("yq", S_[:, L:NR]), cols("Qn", 6 * 256, 7 * 256))], 66e3)
    dma("a", [(a("yq", S_[:, 0:L]), cols("Qw", 0, L))], 33e3)
    return ops


def depend(ops):
    hist = {}
    for i, o in enumerate(ops):
        dep = set()
        for name, lo, hi in o["rd"]:
            psum = name in SCRATCH and SCRATCH[name][0] == "psum"
            for j, l2, h2, w in hist.get(name, ()):
                if l2 < hi and lo < h2 and (w or (psum and ops[j]["eng"] != o["eng"])):
                    dep.add(j)
        for name, lo, hi in o["wr"]:
            if name in ("yx", "yq", "yp", "ym", "LW"):
                dep.update(j for j, l2, h2, w in hist.get(name, ())[:1] if name == "LW")
                continue
            for j, l2, h2, w in hist.get(name, ()):
                if l2 < hi and lo < h2 and not (name == "ADw" and w):
                    dep.add(j)
        for name, lo, hi in o["wr"]:
            keep = [e for e in hist.get(name, ()) if not (lo <= e[1] and e[2] <= hi)]
            hist[name] = keep + [(i, lo, hi, True)]
        for name, lo, hi in o["rd"]:
            hist.setdefault(name, []).append((i, lo, hi, False))
        dep.discard(i)
        o["dep"] = sorted(dep)


def hop(ops, j, i):
    if ops[j]["eng"] == ops[i]["eng"] == "t":
        return -ops[j]["lat"]
    return 0.0 if ops[i]["eng"] == "x" else WAKE


def backward(ops, look):
    n = len(ops)
    rev = [{"eng": o["eng"], "busy": o["busy"], "lat": 0.0, "dep": []} for o in reversed(ops)]
    for i, o in enumerate(ops):
        for j in o["dep"]:
            rev[n - 1 - j]["dep"].append(n - 1 - i)
    for i, o in enumerate(ops):
        if o["lat"] > 100:
            rev[n - 1 - i]["wait"] = o["lat"]
    schedule(rev, look, [ops[n - 1 - i]["start"] for i in range(n)])
    return [rev[n - 1 - i]["start"] + ops[i]["busy"] for i in range(n)]


def refine(ops, look=LOOK, turns=TURNS):
    best = schedule(ops, look)
    for _ in range(turns):
        now = schedule(ops, look, backward(ops, look))
        if now[1] < best[1]:
            best = now
    return best


def schedule(ops, look=LOOK, prio=None):
    n = len(ops)
    succ = [[] for _ in ops]
    for i, o in enumerate(ops):
        for j in o["dep"]:
            succ[j].append(i)
    ahead = [0.0] * n
    for i in range(n - 1, -1, -1):
        ahead[i] = ops[i]["busy"] + ops[i]["lat"] + max([hop(ops, i, k) + ahead[k] for k in succ[i]] + [0.0])
    if prio is not None:
        ahead = prio
    need = [len(o["dep"]) for o in ops]
    ready = [0.0] * n
    pool = {}
    for i, o in enumerate(ops):
        if not need[i]:
            pool.setdefault(o["eng"], []).append(i)
    free, order, end = {}, [], [0.0] * n
    while len(order) < n:
        best = None
        for e, c in pool.items():
            if c:
                t0 = max(free.get(e, 0.0), min(ready[i] for i in c))
                if best is None or t0 < best[0]:
                    best = (t0, e)
        t0, e = best
        i = max((i for i in pool[e] if ready[i] <= t0 + look), key=lambda i: (ahead[i], -i))
        pool[e].remove(i)
        st = max(t0, ready[i])
        ops[i]["start"] = st
        ops[i]["ahead"] = ahead[i]
        free[e] = st + ops[i]["busy"]
        end[i] = free[e] + ops[i]["lat"]
        order.append(i)
        for k in succ[i]:
            ready[k] = max(ready[k], end[i] + hop(ops, i, k) + ops[k].get("wait", 0.0))
            need[k] -= 1
            if not need[k]:
                pool.setdefault(ops[k]["eng"], []).append(k)
    return order, max(end)


def emit(g, T, ops, order):
    queue = {"v": g.vector, "a": g.scalar, "t": g.tensor, "g": g, "s": g.sync}
    total, seen, ndma = {}, {}, [0]
    for i in order:
        o = ops[i]
        e = o["eng"]
        if e == "x":
            o["done"] = o["sem"]
            total[o["sem"][0]] = o["sem"][1]
            continue
        want = {}
        for j in o["dep"]:
            if ops[j]["eng"] == e == "t":
                continue
            s, n = ops[j]["done"]
            want[s] = max(want.get(s, 0), n)
        for s, n in want.items():
            if seen.get((e, s), 0) < n:
                queue[e].wait_ge(T.sem[s], n)
                seen[(e, s)] = n
        if o["dma"]:
            s = "d%d" % ndma[0]
            ndma[0] += 1
            for fn in o["fn"]:
                fn().then_inc(T.sem[s], 16)
            total[s] = 16 * o["dma"]
        elif o["sem"]:
            o["fn"]()
            s = o["sem"][0]
            total[s] = total.get(s, 0) + o["sem"][1]
        else:
            s = e
            o["fn"]().then_inc(T.sem[s], 1)
            total[s] = total.get(s, 0) + 1
        o["done"] = (s, total[s])
    for s, n in total.items():
        g.wait_ge(T.sem[s], n)


def rank_program(g, core, T, topo):
    rank = T.rank_of(core)
    if rank is None:
        return
    ops = build(rank, core, T, topo, g)
    depend(ops)
    order, _ = refine(ops)
    emit(g, T, ops, order)
